import numpy as np, ml_dtypes
CORES = [44,45,46,47,172,173,174,175,300,301,302,303,428,429,430,431]
N = 16
F = 64
def setup_inputs(rng):
    return {"x": rng.standard_normal((N, 128, N * F), dtype=np.float32).astype(ml_dtypes.bfloat16), "w": rng.standard_normal((N, 128, 128), dtype=np.float32).astype(ml_dtypes.bfloat16)}
def setup_inputs_big(rng):
    d = setup_inputs(rng)
    for k in ("x", "w"): d[k] = (d[k].astype(np.float32) * 1024.0).astype(d[k].dtype)
    return d
def setup_inputs_small(rng):
    d = setup_inputs(rng)
    for k in ("x", "w"): d[k] = (d[k].astype(np.float32) * (1 / 1024.0)).astype(d[k].dtype)
    return d
def setup_inputs_apart(rng):
    d = setup_inputs(rng)
    f = (10.0 ** rng.permutation(np.linspace(-1.5, 1.5, N))).astype(np.float32).reshape(N, 1, 1)
    for k in ("x", "w"): d[k] = (d[k].astype(np.float32) * f).astype(d[k].dtype)
    return d
def reference(x, w):
    X, W = x.astype(np.float64), w.astype(np.float64)
    s = X.sum(axis=0)
    o = np.concatenate([W[r].T @ s[:, F * r:F * r + F] for r in range(N)], axis=1).astype(ml_dtypes.bfloat16 if x.dtype != np.float64 else np.float64)
    return {"y": np.broadcast_to(o, (N,) + o.shape)}

@@ -1,0 +1,143 @@
+from concourse.bass import DstId, RemoteDMATransfer
+
+F = 64
+RAWS = 2
+
+SCRATCH = {
+    "xs": ("sbuf", [128, 16 * F], "bfloat16"),
+    "ws": ("sbuf", [128, 128], "bfloat16"),
+    "red": ("sbuf", [128, (3 + RAWS) * 2 * F], "bfloat16"),
+    "acc": ("sbuf", [128, 5 * F], "bfloat16"),
+    "yb": ("sbuf", [128, 16 * F], "bfloat16"),
+    "ps": ("psum", [128, F], "float32"),
+}
+SEMAPHORES = ["ldx", "lds", "ldc", "ldo", "ldw", "redin", "ownin", "r2in", "mm", "cp",
+              "a1", "ao", "fs", "fc", "fx", "sent", "st"]
+
+
+def rank_program(g, core, T, topo):
+    if T.rank_of(core) is None:
+        return
+    sem = T.sem
+    hosts = {}
+    for c in T.cores:
+        hosts.setdefault(topo.host(c), []).append(c)
+    me = topo.host(core)
+    mine = hosts[me]
+    L = len(mine)
+    j = mine.index(core)
+
+    S = C = X = None
+    for h, m in hosts.items():
+        if h == me:
+            continue
+        if not topo.may_write(core, m[j]):
+            X = h
+        elif topo.same_plane(core, m[j]):
+            S = h
+        else:
+            C = h
+    nb = (S, C)
+    kind, pair = j % 2, j // 2
+
+    def role_core(h, k, p):
+        return hosts[h][2 * p + k]
+
+    def cols(h, b, n):
+        a = F * (T.rank_of(hosts[h][0]) + b)
+        return slice(a, a + F * n)
+
+    on_mask, off_mask = topo.mask(core, mine[(j + 1) % L]), topo.mask(core, hosts[S][j])
+    eng = [1 << b for b in range(on_mask.bit_length()) if (on_mask >> b) & 1]
+    lo = [e for e in eng if e & off_mask]
+    hi = [e for e in eng if not e & off_mask]
+    q = len(lo) // 2
+    lo2 = (lo[:q], lo[q:])
+    hq = len(hi) // 2
+    wide = {1: hi[:hq], 2: hi[hq:], 3: None}
+    slim = {1: hi[:hq], 2: hi[hq:hq + hq // 2], 3: hi[hq + hq // 2:]}
+    sent = [0]
+
+    def tr(dst, out, src, engines, rsem):
+        rid, pid = topo.addr(dst, core)
+        sent[0] += len(engines)
+        kw = dict(srcs=src, dsts=[out], alu_op=1) if isinstance(src, list) else dict(src=src, dst=out)
+        return RemoteDMATransfer(dst_ids=[DstId(rid=rid, pnc=pid)], dma_engine_mask=sum(engines), remote_sem=rsem, **kw)
+
+    def peers():
+        return [(o, (j + o) % L) for o in range(1, L)]
+
+    def load(queue, h, s):
+        queue.dma_start(T.xs[:, cols(h, 0, L)], T.x[:, cols(h, 0, L)]).then_inc(s, 16)
+    load(g.sync, X, sem.ldx)
+    load(g.scalar, S, sem.lds)
+    load(g.sync, C, sem.ldc)
+    load(g.scalar, me, sem.ldo)
+    g.sync.dma_start(T.ws[:], T.w[:]).then_inc(sem.ldw, 16)
+
+    g.wait_ge(sem.ldx, 16)
+    slot = 3 + pair
+    g.remote_dma_fused(
+        [tr(role_core(nb[1 - kind], kind, p), T.red[:, slot * 2 * F:(slot + 1) * 2 * F], T.xs[:, cols(X, 2 * p, 2)],
+            lo2[p], sem.redin) for p in range(2)], local_sem=sem.sent)
+
+    g.wait_ge(sem.lds, 16)
+    g.wait_ge(sem.ldc, 16)
+    g.remote_dma_fused(
+        [tr(mine[i], T.red[:, (o - 1) * 2 * F:o * 2 * F], T.xs[:, cols(nb[i % 2], 2 * (i // 2), 2)],
+            wide[o] or lo2[0], sem.redin) for o, i in peers()], local_sem=sem.sent)
+    g.wait_ge(sem.ldo, 16)
+    g.remote_dma_fused(
+        [tr(mine[i], T.acc[:, (o - 1) * F:o * F], T.xs[:, cols(me, i, 1)],
+            wide[o] or lo2[1], sem.ownin) for o, i in peers()], local_sem=sem.sent)
+
+    g.wait_ge(sem.redin, 2 * hq + q + RAWS * q)
+    d = nb[kind]
+    g.remote_dma_fused(
+        [tr(hosts[d][2 * pair + b], T.acc[:, (3 + kind) * F:(4 + kind) * F],
+            [T.xs[:, cols(d, 2 * pair + b, 1)]]
+            + [T.red[:, (2 * s + b) * F:(2 * s + b + 1) * F] for s in range(3 + RAWS)],
+            lo2[b], sem.r2in) for b in range(2)], local_sem=sem.sent)
+
+    own = cols(me, j, 1)
+    t = g.tensor
+    t.wait_ge(sem.ldw, 16)
+    t.wait_ge(sem.ldo, 16)
+    t.matmul(T.ps[:], T.ws[:], T.xs[:, own], True, False)
+    t.wait_ge(sem.ownin, 2 * hq + q)
+    for s in range(3):
+        t.matmul(T.ps[:], T.ws[:], T.acc[:, s * F:(s + 1) * F], False, False)
+    t.wait_ge(sem.r2in, 2 * q)
+    t.matmul(T.ps[:], T.ws[:], T.acc[:, 3 * F:4 * F], False, False)
+    t.matmul(T.ps[:], T.ws[:], T.acc[:, 4 * F:5 * F], False, True).then_inc(sem.mm, 1)
+    g.vector.wait_ge(sem.mm, 1)
+    g.vector.tensor_copy(T.yb[:, own], T.ps[:]).then_inc(sem.cp, 1)
+
+    g.wait_ge(sem.cp, 1)
+    g.remote_dma_fused(
+        [tr(role_core(nb[kk], kk, pair), T.yb[:, own], T.yb[:, own], lo2[kk], sem.a1) for kk in range(2)]
+        + [tr(mine[i], T.yb[:, own], T.yb[:, own], slim[o], sem.ao) for o, i in peers()], local_sem=sem.sent)
+
+    g.wait_ge(sem.a1, 2 * q)
+    pc = cols(d, 2 * pair, 2)
+    g.remote_dma_fused(
+        [tr(hosts[nb[1 - kind]][2 * u + kind], T.yb[:, pc], T.yb[:, pc], lo2[u], sem.fx) for u in range(2)]
+        + [tr(mine[i], T.yb[:, pc], T.yb[:, pc], slim[o], (sem.fs, sem.fc)[kind]) for o, i in peers()],
+        local_sem=sem.sent)
+
+    def store(queue, h):
+        queue.dma_start(T.y[:, cols(h, 0, L)], T.yb[:, cols(h, 0, L)]).then_inc(sem.st, 16)
+    g.sync.wait_ge(sem.cp, 1)
+    g.sync.wait_ge(sem.ao, sum(len(slim[o]) for o in slim))
+    store(g.sync, me)
+    for kk in range(2):
+        if kk == kind:
+            g.scalar.wait_ge(sem.a1, 2 * q)
+        g.scalar.wait_ge((sem.fs, sem.fc)[kk],
+                         sum(len(slim[(j - i) % L]) for i in range(L) if i % 2 == kk and i != j))
+        store(g.scalar, nb[kk])
+    g.sync.wait_ge(sem.fx, 2 * q)
+    store(g.sync, X)
+
+    g.wait_ge(sem.sent, sent[0])
+    g.wait_ge(sem.st, 64)

@@ -1,4 +1,5 @@
 from concourse.bass import DstId, RemoteDMATransfer
+from concourse.mybir import AluOpType
 
 F = 64
 RAWS = 2
@@ -7,11 +8,14 @@ SCRATCH = {
     "xs": ("sbuf", [128, 16 * F], "bfloat16"),
     "ws": ("sbuf", [128, 128], "bfloat16"),
     "red": ("sbuf", [128, (3 + RAWS) * 2 * F], "bfloat16"),
+    "pa": ("sbuf", [128, 2 * F], "bfloat16"),
+    "pb": ("sbuf", [128, 2 * F], "bfloat16"),
+    "pre": ("sbuf", [128, 2 * F], "bfloat16"),
     "acc": ("sbuf", [128, 5 * F], "bfloat16"),
     "yb": ("sbuf", [128, 16 * F], "bfloat16"),
     "ps": ("psum", [128, F], "float32"),
 }
-SEMAPHORES = ["ldx", "lds", "ldc", "ldo", "ldw", "redin", "ownin", "r2in", "mm", "cp",
+SEMAPHORES = ["ldx", "lds", "ldc", "ldo", "ldw", "rs1", "rs23", "rawin", "va", "vp", "ownin", "r2in", "mm", "cp",
               "a1", "ao", "fs", "fc", "fx", "sent", "st"]
 
 
@@ -54,8 +58,8 @@ def rank_program(g, core, T, topo):
     q = len(lo) // 2
     lo2 = (lo[:q], lo[q:])
     hq = len(hi) // 2
-    wide = {1: hi[:hq], 2: hi[hq:], 3: None}
     slim = {1: hi[:hq], 2: hi[hq:hq + hq // 2], 3: hi[hq + hq // 2:]}
+    nslim = sum(len(slim[o]) for o in slim)
     sent = [0]
 
     def tr(dst, out, src, engines, rsem):
@@ -79,24 +83,34 @@ def rank_program(g, core, T, topo):
     slot = 3 + pair
     g.remote_dma_fused(
         [tr(role_core(nb[1 - kind], kind, p), T.red[:, slot * 2 * F:(slot + 1) * 2 * F], T.xs[:, cols(X, 2 * p, 2)],
-            lo2[p], sem.redin) for p in range(2)], local_sem=sem.sent)
+            lo2[p], sem.rawin) for p in range(2)], local_sem=sem.sent)
 
     g.wait_ge(sem.lds, 16)
     g.wait_ge(sem.ldc, 16)
     g.remote_dma_fused(
         [tr(mine[i], T.red[:, (o - 1) * 2 * F:o * 2 * F], T.xs[:, cols(nb[i % 2], 2 * (i // 2), 2)],
-            wide[o] or lo2[0], sem.redin) for o, i in peers()], local_sem=sem.sent)
+            slim[o], sem.rs1 if o == 1 else sem.rs23) for o, i in peers()], local_sem=sem.sent)
     g.wait_ge(sem.ldo, 16)
     g.remote_dma_fused(
         [tr(mine[i], T.acc[:, (o - 1) * F:o * F], T.xs[:, cols(me, i, 1)],
-            wide[o] or lo2[1], sem.ownin) for o, i in peers()], local_sem=sem.sent)
+            slim[o], sem.ownin) for o, i in peers()], local_sem=sem.sent)
 
-    g.wait_ge(sem.redin, 2 * hq + q + RAWS * q)
     d = nb[kind]
+    v = g.vector
+    v.wait_ge((sem.lds, sem.ldc)[kind], 16)
+    v.wait_ge(sem.rs1, len(slim[1]))
+    v.tensor_tensor(T.pa[:], T.xs[:, cols(d, 2 * pair, 2)], T.red[:, 0:2 * F], AluOpType.add).then_inc(sem.va, 1)
+    v.wait_ge(sem.rs23, len(slim[2]) + len(slim[3]))
+    v.tensor_tensor(T.pb[:], T.red[:, 2 * F:4 * F], T.red[:, 4 * F:6 * F], AluOpType.add).then_inc(sem.va, 1)
+    v.wait_ge(sem.va, 2)
+    v.tensor_tensor(T.pre[:], T.pa[:], T.pb[:], AluOpType.add).then_inc(sem.vp, 1)
+
+    g.wait_ge(sem.vp, 1)
+    g.wait_ge(sem.rawin, RAWS * q)
     g.remote_dma_fused(
         [tr(hosts[d][2 * pair + b], T.acc[:, (3 + kind) * F:(4 + kind) * F],
-            [T.xs[:, cols(d, 2 * pair + b, 1)]]
-            + [T.red[:, (2 * s + b) * F:(2 * s + b + 1) * F] for s in range(3 + RAWS)],
+            [T.pre[:, b * F:(b + 1) * F]]
+            + [T.red[:, (2 * s + b) * F:(2 * s + b + 1) * F] for s in range(3, 3 + RAWS)],
             lo2[b], sem.r2in) for b in range(2)], local_sem=sem.sent)
 
     own = cols(me, j, 1)
@@ -104,14 +118,14 @@ def rank_program(g, core, T, topo):
     t.wait_ge(sem.ldw, 16)
     t.wait_ge(sem.ldo, 16)
     t.matmul(T.ps[:], T.ws[:], T.xs[:, own], True, False)
-    t.wait_ge(sem.ownin, 2 * hq + q)
+    t.wait_ge(sem.ownin, nslim)
     for s in range(3):
         t.matmul(T.ps[:], T.ws[:], T.acc[:, s * F:(s + 1) * F], False, False)
     t.wait_ge(sem.r2in, 2 * q)
     t.matmul(T.ps[:], T.ws[:], T.acc[:, 3 * F:4 * F], False, False)
     t.matmul(T.ps[:], T.ws[:], T.acc[:, 4 * F:5 * F], False, True).then_inc(sem.mm, 1)
-    g.vector.wait_ge(sem.mm, 1)
-    g.vector.tensor_copy(T.yb[:, own], T.ps[:]).then_inc(sem.cp, 1)
+    v.wait_ge(sem.mm, 1)
+    v.tensor_copy(T.yb[:, own], T.ps[:]).then_inc(sem.cp, 1)
 
     g.wait_ge(sem.cp, 1)
     g.remote_dma_fused(
@@ -128,7 +142,7 @@ def rank_program(g, core, T, topo):
     def store(queue, h):
         queue.dma_start(T.y[:, cols(h, 0, L)], T.yb[:, cols(h, 0, L)]).then_inc(sem.st, 16)
     g.sync.wait_ge(sem.cp, 1)
-    g.sync.wait_ge(sem.ao, sum(len(slim[o]) for o in slim))
+    g.sync.wait_ge(sem.ao, nslim)
     store(g.sync, me)
     for kk in range(2):
         if kk == kind:

@@ -2,61 +2,70 @@ from concourse.bass import DstId, RemoteDMATransfer
 from concourse.mybir import AluOpType
 
 F = 64
-RAWS = 2
+WORLD = 512
 
 SCRATCH = {
     "xs": ("sbuf", [128, 16 * F], "bfloat16"),
     "ws": ("sbuf", [128, 128], "bfloat16"),
-    "red": ("sbuf", [128, (3 + RAWS) * 2 * F], "bfloat16"),
-    "pa": ("sbuf", [128, 2 * F], "bfloat16"),
-    "pb": ("sbuf", [128, 2 * F], "bfloat16"),
-    "pre": ("sbuf", [128, 2 * F], "bfloat16"),
-    "acc": ("sbuf", [128, 5 * F], "bfloat16"),
+    "red": ("sbuf", [128, 4 * F], "bfloat16"),
+    "rawb": ("sbuf", [128, 2 * F], "bfloat16"),
+    "pa": ("sbuf", [128, F], "bfloat16"),
+    "pb": ("sbuf", [128, F], "bfloat16"),
+    "pre": ("sbuf", [128, F], "bfloat16"),
+    "acc": ("sbuf", [128, 7 * F], "bfloat16"),
     "yb": ("sbuf", [128, 16 * F], "bfloat16"),
     "ps": ("psum", [128, F], "float32"),
 }
-SEMAPHORES = ["ldx", "lds", "ldc", "ldo", "ldw", "rs1", "rs23", "rawin", "va", "vp", "ownin", "r2in", "mm", "cp",
+SEMAPHORES = ["ldx", "lds", "ldc", "ldo", "ldw", "rsin", "rawin", "va", "vp", "ownin", "r2e", "r2in", "mm", "cp",
               "a1", "ao", "fs", "fc", "fx", "sent", "st"]
 
 
 def rank_program(g, core, T, topo):
-    if T.rank_of(core) is None:
-        return
     sem = T.sem
-    hosts = {}
+    ranks = {}
     for c in T.cores:
-        hosts.setdefault(topo.host(c), []).append(c)
+        ranks.setdefault(topo.host(c), []).append(c)
     me = topo.host(core)
-    mine = hosts[me]
+    if me not in ranks or topo.chip(core) != topo.chip(ranks[me][0]):
+        return
+    relays = {}
+    for h, m in ranks.items():
+        relays[h] = m + [c for c in range(WORLD)
+                         if topo.host(c) == h and topo.chip(c) == topo.chip(m[0]) and c not in m]
+    mine = ranks[me]
     L = len(mine)
-    j = mine.index(core)
+    j = relays[me].index(core)
+    is_rank = j < L
+    near = [c for c in mine if c != core]
+    others = [c for c in relays[me] if c not in mine]
 
     S = C = X = None
-    for h, m in hosts.items():
+    for h, m in ranks.items():
         if h == me:
             continue
-        if not topo.may_write(core, m[j]):
+        if not topo.may_write(core, m[0]):
             X = h
-        elif topo.same_plane(core, m[j]):
+        elif topo.same_plane(core, m[0]):
             S = h
         else:
             C = h
     nb = (S, C)
-    kind, pair = j % 2, j // 2
+    kind, blk = j % 2, j // 2
+    d = nb[kind]
 
-    def role_core(h, k, p):
-        return hosts[h][2 * p + k]
+    def relay(h, k, b):
+        return relays[h][2 * b + k]
 
     def cols(h, b, n):
-        a = F * (T.rank_of(hosts[h][0]) + b)
+        a = F * (T.rank_of(ranks[h][0]) + b)
         return slice(a, a + F * n)
 
-    on_mask, off_mask = topo.mask(core, mine[(j + 1) % L]), topo.mask(core, hosts[S][j])
+    on_mask, off_mask = topo.mask(core, near[0]), topo.mask(core, ranks[S][0])
     eng = [1 << b for b in range(on_mask.bit_length()) if (on_mask >> b) & 1]
     lo = [e for e in eng if e & off_mask]
     hi = [e for e in eng if not e & off_mask]
+    lo_side = (lo[0::2], lo[1::2])
     q = len(lo) // 2
-    lo2 = (lo[:q], lo[q:])
     hq = len(hi) // 2
     slim = {1: hi[:hq], 2: hi[hq:hq + hq // 2], 3: hi[hq + hq // 2:]}
     nslim = sum(len(slim[o]) for o in slim)
@@ -71,87 +80,117 @@ def rank_program(g, core, T, topo):
     def peers():
         return [(o, (j + o) % L) for o in range(1, L)]
 
-    def load(queue, h, s):
-        queue.dma_start(T.xs[:, cols(h, 0, L)], T.x[:, cols(h, 0, L)]).then_inc(s, 16)
-    load(g.sync, X, sem.ldx)
-    load(g.scalar, S, sem.lds)
-    load(g.sync, C, sem.ldc)
-    load(g.scalar, me, sem.ldo)
-    g.sync.dma_start(T.ws[:], T.w[:]).then_inc(sem.ldw, 16)
+    v, t = g.vector, g.tensor
+    rawn = q // 2
 
-    g.wait_ge(sem.ldx, 16)
-    slot = 3 + pair
-    g.remote_dma_fused(
-        [tr(role_core(nb[1 - kind], kind, p), T.red[:, slot * 2 * F:(slot + 1) * 2 * F], T.xs[:, cols(X, 2 * p, 2)],
-            lo2[p], sem.rawin) for p in range(2)], local_sem=sem.sent)
+    if is_rank:
+        def load(queue, h, s):
+            queue.dma_start(T.xs[:, cols(h, 0, L)], T.x[:, cols(h, 0, L)]).then_inc(s, 16)
+        load(g.sync, X, sem.ldx)
+        load(g.scalar, S, sem.lds)
+        load(g.sync, C, sem.ldc)
+        load(g.scalar, me, sem.ldo)
+        g.sync.dma_start(T.ws[:], T.w[:]).then_inc(sem.ldw, 16)
 
-    g.wait_ge(sem.lds, 16)
-    g.wait_ge(sem.ldc, 16)
-    g.remote_dma_fused(
-        [tr(mine[i], T.red[:, (o - 1) * 2 * F:o * 2 * F], T.xs[:, cols(nb[i % 2], 2 * (i // 2), 2)],
-            slim[o], sem.rs1 if o == 1 else sem.rs23) for o, i in peers()], local_sem=sem.sent)
-    g.wait_ge(sem.ldo, 16)
-    g.remote_dma_fused(
-        [tr(mine[i], T.acc[:, (o - 1) * F:o * F], T.xs[:, cols(me, i, 1)],
-            slim[o], sem.ownin) for o, i in peers()], local_sem=sem.sent)
+        g.wait_ge(sem.ldx, 16)
+        trs, used = [], [0, 0]
+        for b in range(L):
+            side = (j + b) % 2
+            e = lo_side[side][used[side] * rawn:(used[side] + 1) * rawn]
+            used[side] += 1
+            trs.append(tr(relay(nb[side], 1 - side, b), T.rawb[:, (j // 2) * F:(j // 2 + 1) * F],
+                          T.xs[:, cols(X, b, 1)], e, sem.rawin))
+        g.remote_dma_fused(trs, local_sem=sem.sent)
 
-    d = nb[kind]
-    v = g.vector
-    v.wait_ge((sem.lds, sem.ldc)[kind], 16)
-    v.wait_ge(sem.rs1, len(slim[1]))
-    v.tensor_tensor(T.pa[:], T.xs[:, cols(d, 2 * pair, 2)], T.red[:, 0:2 * F], AluOpType.add).then_inc(sem.va, 1)
-    v.wait_ge(sem.rs23, len(slim[2]) + len(slim[3]))
-    v.tensor_tensor(T.pb[:], T.red[:, 2 * F:4 * F], T.red[:, 4 * F:6 * F], AluOpType.add).then_inc(sem.va, 1)
-    v.wait_ge(sem.va, 2)
-    v.tensor_tensor(T.pre[:], T.pa[:], T.pb[:], AluOpType.add).then_inc(sem.vp, 1)
+        def role_cols(c):
+            r = relays[me].index(c)
+            return cols(nb[r % 2], r // 2, 1)
+        mycol = T.red[:, j * F:(j + 1) * F]
+        g.wait_ge(sem.lds, 16)
+        g.wait_ge(sem.ldc, 16)
+        g.remote_dma_fused(
+            [tr(c, mycol, T.xs[:, role_cols(c)], hi[2 * n:2 * n + 2], sem.rsin) for n, c in enumerate(others)],
+            local_sem=sem.sent)
+        g.remote_dma_fused(
+            [tr(mine[i], mycol, T.xs[:, role_cols(mine[i])], slim[o], sem.rsin) for o, i in peers()],
+            local_sem=sem.sent)
+        g.wait_ge(sem.ldo, 16)
+        g.remote_dma_fused(
+            [tr(mine[i], T.acc[:, (o - 1) * F:o * F], T.xs[:, cols(me, i, 1)],
+                slim[o], sem.ownin) for o, i in peers()], local_sem=sem.sent)
 
-    g.wait_ge(sem.vp, 1)
-    g.wait_ge(sem.rawin, RAWS * q)
-    g.remote_dma_fused(
-        [tr(hosts[d][2 * pair + b], T.acc[:, (3 + kind) * F:(4 + kind) * F],
-            [T.pre[:, b * F:(b + 1) * F]]
-            + [T.red[:, (2 * s + b) * F:(2 * s + b + 1) * F] for s in range(3, 3 + RAWS)],
-            lo2[b], sem.r2in) for b in range(2)], local_sem=sem.sent)
+        o3 = [i for i in range(L) if i != j]
+        v.wait_ge((sem.lds, sem.ldc)[kind], 16)
+        v.wait_ge(sem.rsin, nslim)
+        v.tensor_tensor(T.pa[:], T.xs[:, cols(d, blk, 1)], T.red[:, o3[0] * F:(o3[0] + 1) * F],
+                        AluOpType.add).then_inc(sem.va, 1)
+        v.tensor_tensor(T.pb[:], T.red[:, o3[1] * F:(o3[1] + 1) * F], T.red[:, o3[2] * F:(o3[2] + 1) * F],
+                        AluOpType.add).then_inc(sem.va, 1)
+        v.wait_ge(sem.va, 2)
+        v.tensor_tensor(T.pre[:], T.pa[:], T.pb[:], AluOpType.add).then_inc(sem.vp, 1)
 
-    own = cols(me, j, 1)
-    t = g.tensor
-    t.wait_ge(sem.ldw, 16)
-    t.wait_ge(sem.ldo, 16)
-    t.matmul(T.ps[:], T.ws[:], T.xs[:, own], True, False)
-    t.wait_ge(sem.ownin, nslim)
-    for s in range(3):
-        t.matmul(T.ps[:], T.ws[:], T.acc[:, s * F:(s + 1) * F], False, False)
-    t.wait_ge(sem.r2in, 2 * q)
-    t.matmul(T.ps[:], T.ws[:], T.acc[:, 3 * F:4 * F], False, False)
-    t.matmul(T.ps[:], T.ws[:], T.acc[:, 4 * F:5 * F], False, True).then_inc(sem.mm, 1)
-    v.wait_ge(sem.mm, 1)
-    v.tensor_copy(T.yb[:, own], T.ps[:]).then_inc(sem.cp, 1)
+    owner = ranks[d][blk]
+    raws = [T.rawb[:, s * F:(s + 1) * F] for s in range(2)]
+    main = T.acc[:, (3 + kind) * F:(4 + kind) * F]
+    if is_rank:
+        g.wait_ge(sem.vp, 1)
+        g.wait_ge(sem.rawin, 2 * rawn)
+        g.remote_dma_fused([tr(owner, main, [T.pre[:]] + raws, lo, sem.r2in)], local_sem=sem.sent)
+    else:
+        g.wait_ge(sem.rsin, 2 * L)
+        g.remote_dma_fused([tr(owner, T.acc[:, (5 + kind) * F:(6 + kind) * F],
+                               [T.red[:, s * F:(s + 1) * F] for s in range(L)], lo, sem.r2e)], local_sem=sem.sent)
+        g.wait_ge(sem.rawin, 2 * rawn)
+        g.remote_dma_fused([tr(owner, main, raws, lo, sem.r2in)], local_sem=sem.sent)
 
-    g.wait_ge(sem.cp, 1)
-    g.remote_dma_fused(
-        [tr(role_core(nb[kk], kk, pair), T.yb[:, own], T.yb[:, own], lo2[kk], sem.a1) for kk in range(2)]
-        + [tr(mine[i], T.yb[:, own], T.yb[:, own], slim[o], sem.ao) for o, i in peers()], local_sem=sem.sent)
+    if is_rank:
+        own = cols(me, j, 1)
+        t.wait_ge(sem.ldw, 16)
+        t.wait_ge(sem.ldo, 16)
+        t.matmul(T.ps[:], T.ws[:], T.xs[:, own], True, False)
+        t.wait_ge(sem.ownin, nslim)
+        for s in range(3):
+            t.matmul(T.ps[:], T.ws[:], T.acc[:, s * F:(s + 1) * F], False, False)
+        if 2 * j >= L:
+            t.wait_ge(sem.r2e, 2 * len(lo))
+            for s in (5, 6):
+                t.matmul(T.ps[:], T.ws[:], T.acc[:, s * F:(s + 1) * F], False, False)
+        t.wait_ge(sem.r2in, 2 * len(lo))
+        t.matmul(T.ps[:], T.ws[:], T.acc[:, 3 * F:4 * F], False, False)
+        t.matmul(T.ps[:], T.ws[:], T.acc[:, 4 * F:5 * F], False, True).then_inc(sem.mm, 1)
+        v.wait_ge(sem.mm, 1)
+        v.tensor_copy(T.yb[:, own], T.ps[:]).then_inc(sem.cp, 1)
 
-    g.wait_ge(sem.a1, 2 * q)
-    pc = cols(d, 2 * pair, 2)
-    g.remote_dma_fused(
-        [tr(hosts[nb[1 - kind]][2 * u + kind], T.yb[:, pc], T.yb[:, pc], lo2[u], sem.fx) for u in range(2)]
-        + [tr(mine[i], T.yb[:, pc], T.yb[:, pc], slim[o], (sem.fs, sem.fc)[kind]) for o, i in peers()],
-        local_sem=sem.sent)
+        g.wait_ge(sem.cp, 1)
+        g.remote_dma_fused(
+            [tr(relay(nb[kk], kk, j), T.yb[:, own], T.yb[:, own], lo_side[kk], sem.a1) for kk in range(2)]
+            + [tr(mine[i], T.yb[:, own], T.yb[:, own], slim[o], sem.ao) for o, i in peers()], local_sem=sem.sent)
 
-    def store(queue, h):
-        queue.dma_start(T.y[:, cols(h, 0, L)], T.yb[:, cols(h, 0, L)]).then_inc(sem.st, 16)
-    g.sync.wait_ge(sem.cp, 1)
-    g.sync.wait_ge(sem.ao, nslim)
-    store(g.sync, me)
-    for kk in range(2):
-        if kk == kind:
-            g.scalar.wait_ge(sem.a1, 2 * q)
-        g.scalar.wait_ge((sem.fs, sem.fc)[kk],
-                         sum(len(slim[(j - i) % L]) for i in range(L) if i % 2 == kk and i != j))
-        store(g.scalar, nb[kk])
-    g.sync.wait_ge(sem.fx, 2 * q)
-    store(g.sync, X)
+    g.wait_ge(sem.a1, q)
+    bc = cols(d, blk, 1)
+    off = [tr(ranks[nb[1 - kind]][2 * u + kind], T.yb[:, bc], T.yb[:, bc], lo[u * q:(u + 1) * q], sem.fx)
+           for u in range(2)]
+    on = [tr(c, T.yb[:, bc], T.yb[:, bc], hi[2 * n:2 * n + 2], (sem.fs, sem.fc)[kind]) for n, c in enumerate(near)]
+    if is_rank:
+        g.remote_dma_fused(off + on, local_sem=sem.sent)
+    else:
+        g.remote_dma_fused(off, local_sem=sem.sent)
+        g.remote_dma_fused(on, local_sem=sem.sent)
+
+    if is_rank:
+        def store(queue, h):
+            queue.dma_start(T.y[:, cols(h, 0, L)], T.yb[:, cols(h, 0, L)]).then_inc(sem.st, 16)
+        g.sync.wait_ge(sem.cp, 1)
+        g.sync.wait_ge(sem.ao, nslim)
+        store(g.sync, me)
+        for kk in range(2):
+            if kk == kind:
+                g.scalar.wait_ge(sem.a1, q)
+            g.scalar.wait_ge((sem.fs, sem.fc)[kk], 2 * (L - (1 if kk == kind else 0)))
+            store(g.scalar, nb[kk])
+        g.sync.wait_ge(sem.fx, L * q)
+        store(g.sync, X)
 
     g.wait_ge(sem.sent, sent[0])
-    g.wait_ge(sem.st, 64)
+    if is_rank:
+        g.wait_ge(sem.st, 64)

from concourse.bass import DstId, RemoteDMATransfer
from concourse.mybir import AluOpType

F = 64
WORLD = 512

SCRATCH = {
    "xs": ("sbuf", [128, 16 * F], "bfloat16"),
    "ws": ("sbuf", [128, 128], "bfloat16"),
    "red": ("sbuf", [128, 4 * F], "bfloat16"),
    "rawb": ("sbuf", [128, 2 * F], "bfloat16"),
    "pa": ("sbuf", [128, F], "bfloat16"),
    "pb": ("sbuf", [128, F], "bfloat16"),
    "pre": ("sbuf", [128, F], "bfloat16"),
    "acc": ("sbuf", [128, 7 * F], "bfloat16"),
    "yb": ("sbuf", [128, 16 * F], "bfloat16"),
    "ps": ("psum", [128, F], "float32"),
}
SEMAPHORES = ["ldx", "lds", "ldc", "ldo", "ldw", "rsin", "rawin", "va", "vp", "ownin", "r2e", "r2in", "mm", "cp",
              "a1", "ao", "fs", "fc", "fx", "sent", "st"]


def rank_program(g, core, T, topo):
    sem = T.sem
    ranks = {}
    for c in T.cores:
        ranks.setdefault(topo.host(c), []).append(c)
    me = topo.host(core)
    if me not in ranks or topo.chip(core) != topo.chip(ranks[me][0]):
        return
    relays = {}
    for h, m in ranks.items():
        relays[h] = m + [c for c in range(WORLD)
                         if topo.host(c) == h and topo.chip(c) == topo.chip(m[0]) and c not in m]
    mine = ranks[me]
    L = len(mine)
    j = relays[me].index(core)
    is_rank = j < L
    near = [c for c in mine if c != core]
    others = [c for c in relays[me] if c not in mine]

    S = C = X = None
    for h, m in ranks.items():
        if h == me:
            continue
        if not topo.may_write(core, m[0]):
            X = h
        elif topo.same_plane(core, m[0]):
            S = h
        else:
            C = h
    nb = (S, C)
    kind, blk = j % 2, j // 2
    d = nb[kind]

    def relay(h, k, b):
        return relays[h][2 * b + k]

    def cols(h, b, n):
        a = F * (T.rank_of(ranks[h][0]) + b)
        return slice(a, a + F * n)

    on_mask, off_mask = topo.mask(core, near[0]), topo.mask(core, ranks[S][0])
    eng = [1 << b for b in range(on_mask.bit_length()) if (on_mask >> b) & 1]
    lo = [e for e in eng if e & off_mask]
    hi = [e for e in eng if not e & off_mask]
    lo_side = (lo[0::2], lo[1::2])
    q = len(lo) // 2
    hq = len(hi) // 2
    slim = {1: hi[:hq], 2: hi[hq:hq + hq // 2], 3: hi[hq + hq // 2:]}
    nslim = sum(len(slim[o]) for o in slim)
    sent = [0]

    def tr(dst, out, src, engines, rsem):
        rid, pid = topo.addr(dst, core)
        sent[0] += len(engines)
        kw = dict(srcs=src, dsts=[out], alu_op=1) if isinstance(src, list) else dict(src=src, dst=out)
        return RemoteDMATransfer(dst_ids=[DstId(rid=rid, pnc=pid)], dma_engine_mask=sum(engines), remote_sem=rsem, **kw)

    def peers():
        return [(o, (j + o) % L) for o in range(1, L)]

    v, t = g.vector, g.tensor
    rawn = q // 2

    if is_rank:
        def load(queue, h, s):
            queue.dma_start(T.xs[:, cols(h, 0, L)], T.x[:, cols(h, 0, L)]).then_inc(s, 16)
        load(g.sync, X, sem.ldx)
        load(g.scalar, S, sem.lds)
        load(g.sync, C, sem.ldc)
        load(g.scalar, me, sem.ldo)
        g.sync.dma_start(T.ws[:], T.w[:]).then_inc(sem.ldw, 16)

        g.wait_ge(sem.ldx, 16)
        trs, used = [], [0, 0]
        for b in range(L):
            side = (j + b) % 2
            e = lo_side[side][used[side] * rawn:(used[side] + 1) * rawn]
            used[side] += 1
            trs.append(tr(relay(nb[side], 1 - side, b), T.rawb[:, (j // 2) * F:(j // 2 + 1) * F],
                          T.xs[:, cols(X, b, 1)], e, sem.rawin))
        g.remote_dma_fused(trs, local_sem=sem.sent)

        def role_cols(c):
            r = relays[me].index(c)
            return cols(nb[r % 2], r // 2, 1)
        mycol = T.red[:, j * F:(j + 1) * F]
        g.wait_ge(sem.lds, 16)
        g.wait_ge(sem.ldc, 16)
        g.remote_dma_fused(
            [tr(c, mycol, T.xs[:, role_cols(c)], hi[2 * n:2 * n + 2], sem.rsin) for n, c in enumerate(others)],
            local_sem=sem.sent)
        g.remote_dma_fused(
            [tr(mine[i], mycol, T.xs[:, role_cols(mine[i])], slim[o], sem.rsin) for o, i in peers()],
            local_sem=sem.sent)
        g.wait_ge(sem.ldo, 16)
        g.remote_dma_fused(
            [tr(mine[i], T.acc[:, (o - 1) * F:o * F], T.xs[:, cols(me, i, 1)],
                slim[o], sem.ownin) for o, i in peers()], local_sem=sem.sent)

        o3 = [i for i in range(L) if i != j]
        v.wait_ge((sem.lds, sem.ldc)[kind], 16)
        v.wait_ge(sem.rsin, nslim)
        v.tensor_tensor(T.pa[:], T.xs[:, cols(d, blk, 1)], T.red[:, o3[0] * F:(o3[0] + 1) * F],
                        AluOpType.add).then_inc(sem.va, 1)
        v.tensor_tensor(T.pb[:], T.red[:, o3[1] * F:(o3[1] + 1) * F], T.red[:, o3[2] * F:(o3[2] + 1) * F],
                        AluOpType.add).then_inc(sem.va, 1)
        v.wait_ge(sem.va, 2)
        v.tensor_tensor(T.pre[:], T.pa[:], T.pb[:], AluOpType.add).then_inc(sem.vp, 1)

    owner = ranks[d][blk]
    raws = [T.rawb[:, s * F:(s + 1) * F] for s in range(2)]
    main = T.acc[:, (3 + kind) * F:(4 + kind) * F]
    if is_rank:
        g.wait_ge(sem.vp, 1)
        g.wait_ge(sem.rawin, 2 * rawn)
        g.remote_dma_fused([tr(owner, main, [T.pre[:]] + raws, lo, sem.r2in)], local_sem=sem.sent)
    else:
        g.wait_ge(sem.rsin, 2 * L)
        g.remote_dma_fused([tr(owner, T.acc[:, (5 + kind) * F:(6 + kind) * F],
                               [T.red[:, s * F:(s + 1) * F] for s in range(L)], lo, sem.r2e)], local_sem=sem.sent)
        g.wait_ge(sem.rawin, 2 * rawn)
        g.remote_dma_fused([tr(owner, main, raws, lo, sem.r2in)], local_sem=sem.sent)

    if is_rank:
        own = cols(me, j, 1)
        t.wait_ge(sem.ldw, 16)
        t.wait_ge(sem.ldo, 16)
        t.matmul(T.ps[:], T.ws[:], T.xs[:, own], True, False)
        t.wait_ge(sem.ownin, nslim)
        for s in range(3):
            t.matmul(T.ps[:], T.ws[:], T.acc[:, s * F:(s + 1) * F], False, False)
        if 2 * j >= L:
            t.wait_ge(sem.r2e, 2 * len(lo))
            for s in (5, 6):
                t.matmul(T.ps[:], T.ws[:], T.acc[:, s * F:(s + 1) * F], False, False)
        t.wait_ge(sem.r2in, 2 * len(lo))
        t.matmul(T.ps[:], T.ws[:], T.acc[:, 3 * F:4 * F], False, False)
        t.matmul(T.ps[:], T.ws[:], T.acc[:, 4 * F:5 * F], False, True).then_inc(sem.mm, 1)
        v.wait_ge(sem.mm, 1)
        v.tensor_copy(T.yb[:, own], T.ps[:]).then_inc(sem.cp, 1)

        g.wait_ge(sem.cp, 1)
        g.remote_dma_fused(
            [tr(relay(nb[kk], kk, j), T.yb[:, own], T.yb[:, own], lo_side[kk], sem.a1) for kk in range(2)]
            + [tr(mine[i], T.yb[:, own], T.yb[:, own], slim[o], sem.ao) for o, i in peers()], local_sem=sem.sent)

    g.wait_ge(sem.a1, q)
    bc = cols(d, blk, 1)
    off = [tr(ranks[nb[1 - kind]][2 * u + kind], T.yb[:, bc], T.yb[:, bc], lo[u * q:(u + 1) * q], sem.fx)
           for u in range(2)]
    on = [tr(c, T.yb[:, bc], T.yb[:, bc], hi[2 * n:2 * n + 2], (sem.fs, sem.fc)[kind]) for n, c in enumerate(near)]
    if is_rank:
        g.remote_dma_fused(off + on, local_sem=sem.sent)
    else:
        g.remote_dma_fused(off, local_sem=sem.sent)
        g.remote_dma_fused(on, local_sem=sem.sent)

    if is_rank:
        def store(queue, h):
            queue.dma_start(T.y[:, cols(h, 0, L)], T.yb[:, cols(h, 0, L)]).then_inc(sem.st, 16)
        g.sync.wait_ge(sem.cp, 1)
        g.sync.wait_ge(sem.ao, nslim)
        store(g.sync, me)
        for kk in range(2):
            if kk == kind:
                g.scalar.wait_ge(sem.a1, q)
            g.scalar.wait_ge((sem.fs, sem.fc)[kk], 2 * (L - (1 if kk == kind else 0)))
            store(g.scalar, nb[kk])
        g.sync.wait_ge(sem.fx, L * q)
        store(g.sync, X)

    g.wait_ge(sem.sent, sent[0])
    if is_rank:
        g.wait_ge(sem.st, 64)
